import numpy as np
import ml_dtypes


def mxq(x, axis, fmt="e4m3"):
    dtype, down = {"e4m3": (ml_dtypes.float8_e4m3fn, 7), "e5m2": (ml_dtypes.float8_e5m2, 14)}[fmt]
    v = np.moveaxis(np.asarray(x, np.float32).astype(ml_dtypes.bfloat16).astype(np.float64), axis, -1)
    blocks = v.reshape(v.shape[:-1] + (-1, 32))
    amax = np.abs(blocks).max(-1, keepdims=True)
    byte = np.maximum(np.where(amax > 0, np.frexp(amax)[1] - 1 + 127, 0) - down, 1)
    scale = np.exp2(byte - 127.0)
    codes = (blocks / scale).astype(np.float32).astype(dtype).astype(np.float64)
    return np.moveaxis((codes * scale).reshape(v.shape), -1, axis)


WIDE = False


def mx_kscale(k):
    if not WIDE:
        return np.ones(k)
    levels = np.array([10, -10, 5, -5, 0])
    if k % 512:
        return np.exp2(np.random.permutation(np.resize(levels, k // 32))).repeat(32)
    a = np.empty((k // 512, 16))
    for p in range(k // 512):
        a[p, :8] = np.random.permutation(np.resize(levels, 8))
        for g in range(8):
            far = levels[np.abs(levels - a[p, g]) >= 10]
            a[p, g + 8] = far[np.random.randint(len(far))]
    return np.exp2(a.ravel()).repeat(32)


def f64(x):
    return np.asarray(x).astype(np.float64)


def striped(idx):
    return np.tile(idx.reshape(-1, 16).T, (8, 1)).astype(np.uint16)


def unstriped(offs):
    return offs[:16].T.reshape(-1).astype(np.int64)


def striped8(idx):
    return np.concatenate([x.reshape(-1, 16).T for x in idx]).astype(np.uint16)


def runs(offs, k):
    lists = np.stack([offs[16 * r : 16 * r + 16].T.reshape(-1) for r in range(8)]).astype(np.int64)
    return lists[np.arange(k) % 512 // 64]


def pack_weight(w):
    k, n = w.shape
    w = f64(np.asarray(w, np.float32).astype(ml_dtypes.bfloat16)).reshape(k // 32, 32, n)
    amax = np.abs(w).max(1)
    byte = np.clip(np.where(amax > 0, np.frexp(amax)[1] - 1 + 127 - 7, 1), 1, 254)
    scaled = (w * np.exp2(127.0 - byte)[:, None, :]).reshape(k, n).astype(np.float32)
    words = np.ascontiguousarray(scaled.reshape(k // 512, 128, 4, n).transpose(0, 1, 3, 2)).astype(ml_dtypes.float8_e4m3fn).view(np.uint8)
    return words, np.ascontiguousarray(byte.astype(np.uint8).reshape(k // 512, 16, n))


def unpack_weight(words, scales):
    g, p, n, _ = words.shape
    vals = np.ascontiguousarray(words).view(ml_dtypes.float8_e4m3fn).astype(np.float64) * np.repeat(np.exp2(scales.astype(np.float64) - 127.0), 8, axis=1)[..., None]
    return vals.transpose(0, 1, 3, 2).reshape(g * 512, n)


def sigmoid(v):
    return 1.0 / (1.0 + np.exp(-np.maximum(v, -700.0)))


K, T, S, N, H, W = 512, 2048, 512, 512, 512, 256


def setup_inputs():
    n = np.random.standard_normal
    s = mx_kscale(K)[:, None]
    u = mx_kscale(H)
    packed_xT = pack_weight(n((K, T)) * s)
    perm = np.stack([np.random.permutation(S) for _ in range(8)])
    return {
        "x_words": packed_xT[0],
        "x_scales": packed_xT[1],
        "w1": (n((K, H)) / np.sqrt(K) / s).astype(np.float32),
        "gn": (np.random.uniform(0.5, 1.5, (H, 1)) * u[:, None]).astype(np.float32),
        "w2": (n((H, N)) / np.sqrt(H) / u[:, None]).astype(np.float32),
        "offs": striped(np.random.permutation(T)[:S]),
        "n1": striped8(perm[:, :W]),
        "n2": striped8(perm[:, W:]),
        "n3": striped8(np.stack([np.random.permutation(S) for _ in range(8)])),
        "n4": striped8(np.stack([np.random.permutation(S) for _ in range(8)])),
    }


def reference(x_words, x_scales, w1, gn, w2, offs, n1, n2, n3, n4):
    xq = unpack_weight(x_words, x_scales)[:, unstriped(offs)]
    y = mxq(f64(w1), 0, "e4m3").T @ xq
    pa = y[np.arange(H)[:, None], runs(n1, H)]
    pb = y[np.arange(H)[:, None], runs(n2, H)]
    ra = pa * sigmoid(pb)
    ds = y.copy()
    ds[np.arange(H)[:, None], runs(n2, H)] = ra
    z = f64(gn) * ds
    h = mxq(f64(w2), 0, "e4m3").T @ mxq(z, 0, "e4m3")
    return 0.75 * (h * (y[np.arange(H)[:, None], runs(n4, H)]) - ((h[np.arange(N)[:, None], runs(n3, N)]) * y))

@@ -1,0 +1,203 @@
+from contextlib import ExitStack
+
+import concourse.mybir as mybir
+
+K, T, S, H, N, W = 512, 2048, 512, 512, 512, 256
+FLOPS = 2 * K * H * S + 2 * H * N * S
+
+F32 = mybir.dt.float32
+BF16 = mybir.dt.bfloat16
+I32 = mybir.dt.int32
+U32 = mybir.dt.uint32
+U16 = mybir.dt.uint16
+U8 = mybir.dt.uint8
+FP8X4 = mybir.dt.float8_e4m3fn_x4
+MULT = mybir.AluOpType.mult
+SUB = mybir.AluOpType.subtract
+COPY = mybir.ActivationFunctionType.Copy
+SIGMOID = mybir.ActivationFunctionType.Sigmoid
+
+P = 128
+PACK = 4
+HALF = S // 2
+PER_COL = 16
+
+
+def tile_picked_skipcrossbfold_none_p_kernel(tc, x_words, x_scales, w1, gn, w2, offs, n1, n2, n3, n4, out):
+    nc = tc.nc
+    with ExitStack() as ctx:
+        lists = ctx.enter_context(tc.tile_pool(name="lists", bufs=1))
+        sb = ctx.enter_context(tc.tile_pool(name="sb", bufs=1))
+        ps = ctx.enter_context(tc.psum_pool(name="ps", bufs=1))
+
+        def cols(h):
+            return slice(h * HALF, (h + 1) * HALF)
+
+        def entries(lst, h):
+            return lst[:, h * HALF // PER_COL : (h + 1) * HALF // PER_COL]
+
+        warm = sb.tile([P, 2], F32, name="warm")
+        nc.vector.memset(warm[:, 0:1], 0.0)
+        nc.scalar.activation(warm[:, 1:2], warm[:, 0:1], SIGMOID)
+
+        def load_half(w, h):
+            raw = sb.tile([P, PACK, HALF], F32, name="raw", tag=f"raw{h}")
+            nc.sync.dma_start(raw[:], w.rearrange("(p j) c -> p j c", j=PACK)[:, :, cols(h)])
+            return raw
+
+        def load_list(src, name):
+            lst = lists.tile(list(src.shape), U16, name=name)
+            nc.sync.dma_start(lst[:], src)
+            return lst
+
+        scale_table = sb.tile([P, T], U8, name="scale_table")
+        nc.vector.memset(scale_table[:].bitcast(I32), 0)
+        w1_raw = [load_half(w1, 0)]
+        for q in range(4):
+            nc.sync.dma_start(scale_table[32 * q : 32 * q + 4, :].bitcast(I32), x_scales[0, 4 * q : 4 * q + 4, :].bitcast(I32))
+        offs_t = load_list(offs, "offs_t")
+        w1_raw.append(load_half(w1, 1))
+        word_table = sb.tile([P, T], I32, name="word_table")
+        nc.sync.dma_start(word_table[:], x_words[0].rearrange("p n r -> p (n r)").bitcast(I32))
+        n2_t = load_list(n2, "n2_t")
+        n1_t = load_list(n1, "n1_t")
+        gain = sb.tile([P, PACK], F32, name="gain")
+        nc.sync.dma_start(gain[:], gn.rearrange("(p t) o -> p (t o)", t=PACK))
+        n4_t = load_list(n4, "n4_t")
+        n3_t = load_list(n3, "n3_t")
+
+        def deal(copy, grouped, m0, raw):
+            count = raw.shape[2] // PACK
+            copy(grouped[:, :, m0 : m0 + count, :].rearrange("p t m j -> p m j t"), raw.rearrange("p j (m t) -> p m j t", t=PACK))
+
+        def quantize(codes, scales, values):
+            nc.vector.quantize_mx(out=codes.bitcast(FP8X4), scales=scales, in_=values)
+
+        def product(acc, w_codes, w_scales, t, codes, scales):
+            m = slice(t * P, (t + 1) * P)
+            nc.tensor.matmul_mx(out=acc, lhsT=w_codes[:, m].bitcast(FP8X4), lhsT_scale=w_scales[:, m],
+                                rhs=codes.bitcast(FP8X4), rhs_scale=scales, start=True, stop=True)
+
+        x_codes = sb.tile([P, S], U32, name="x_codes", align_bytes=64)
+        x_bytes = sb.tile([P, S], U8, name="x_bytes", align_bytes=64)
+        nc.vector.tensor_copy(x_bytes[:], scale_table[:].indirect(offs_t[:]))
+        w1_grouped = sb.tile([P, PACK, P, PACK], BF16, name="w1_grouped", align_bytes=64)
+        deal(nc.scalar.copy, w1_grouped, 0, w1_raw[0][:])
+        deal(nc.vector.tensor_copy, w1_grouped, P // 2, w1_raw[1][:])
+        w1_codes = sb.tile([P, H], U32, name="w1_codes", align_bytes=64)
+        w1_scales = sb.tile([P, H], U8, name="w1_scales", align_bytes=64)
+        quantize(w1_codes[:], w1_scales[:], w1_grouped[:].rearrange("p t m j -> p (t m j)"))
+
+        w2_raw = [load_half(w2, h) for h in range(2)]
+
+        shared = [ps.tile([P, S], F32, name=f"shared{h}") for h in range(2)]
+        y_banks = [[shared[h][:, cols(0)] for h in range(2)]] + [ps.tile([P, S], F32, name=f"y_bank{t}") for t in range(1, PACK)]
+        h_banks = [[shared[h][:, cols(1)] for h in range(2)]] + [ps.tile([P, S], F32, name=f"h_bank{t}") for t in range(1, PACK)]
+
+        ds = [sb.tile([P, S], F32, name=f"ds{t}") for t in range(PACK)]
+        y = [sb.tile([P, S], F32, name=f"y{t}") for t in range(PACK)]
+        for h in range(2):
+            nc.vector.tensor_copy(x_codes[:, cols(h)], word_table[:].bitcast(U32).indirect(entries(offs_t, h)))
+            product(y_banks[0][h], w1_codes, w1_scales, 0, x_codes[:, cols(h)], x_bytes[:, cols(h)])
+            nc.scalar.copy(ds[0][:, cols(h)], y_banks[0][h])
+        for t in range(1, PACK):
+            product(y_banks[t][:], w1_codes, w1_scales, t, x_codes[:], x_bytes[:])
+
+        def empty(dst, banks, t, scale):
+            if t == 0:
+                for h in range(2):
+                    nc.scalar.activation(dst[:, cols(h)], banks[0][h], COPY, scale=scale)
+            else:
+                nc.scalar.activation(dst[:], banks[t][:], COPY, scale=scale)
+
+        gate = [sb.tile([P, W], F32, name=f"gate{t}") for t in range(PACK)]
+        pa = [sb.tile([P, W], F32, name=f"pa{t}") for t in range(PACK)]
+        z_flat = sb.tile([P, PACK * S], BF16, name="z_flat")
+        z_pairs = z_flat[:].rearrange("p (h u j e) -> p h u j e", h=2, u=2, e=2)
+        w2_grouped = sb.tile([P, PACK, P, PACK], BF16, name="w2_grouped", align_bytes=64)
+        w2_codes = sb.tile([P, N], U32, name="w2_codes", align_bytes=64)
+        w2_scales = sb.tile([P, N], U8, name="w2_scales", align_bytes=64)
+
+        def fetch(t):
+            if t > 0:
+                empty(ds[t], y_banks, t, 1.0)
+            nc.scalar.activation(gate[t][:], ds[t][:].indirect(n2_t[:]), SIGMOID)
+            nc.vector.tensor_copy(pa[t][:], ds[t][:].indirect(n1_t[:]))
+
+        def put(t):
+            nc.vector.tensor_tensor(ds[t][:].indirect(n2_t[:]), pa[t][:], gate[t][:], MULT)
+
+        def cast(t):
+            if t < PACK - 1:
+                nc.scalar.activation(z_pairs[:, :, t // 2, :, t % 2], ds[t][:].rearrange("p (h j) -> p h j", h=2), COPY, scale=gain[:, t : t + 1])
+            else:
+                for h in range(2):
+                    nc.scalar.activation(z_pairs[:, h, t // 2, :, t % 2], ds[t][:, cols(h)], COPY, scale=gain[:, t : t + 1])
+
+        def deal_w2(q):
+            deal(nc.scalar.copy, w2_grouped, q * 32, w2_raw[q // 2][:, :, (q % 2) * P : (q % 2 + 1) * P])
+
+        fetch(0)
+        put(0)
+        fetch(1)
+        fetch(2)
+        cast(0)
+        put(1)
+        fetch(3)
+        deal_w2(0)
+        cast(1)
+        deal_w2(1)
+        put(2)
+        deal_w2(2)
+        cast(2)
+        deal_w2(3)
+        put(3)
+        cast(3)
+        empty(y[0], y_banks, 0, 1.0)
+        quantize(w2_codes[:], w2_scales[:], w2_grouped[:].rearrange("p t m j -> p (t m j)"))
+
+        z_grouped = [sb.tile([P, HALF, 2], I32, name=f"z_grouped{h}", align_bytes=64) for h in range(2)]
+        z_codes = sb.tile([P, S], U32, name="z_codes", align_bytes=64)
+        z_scales = sb.tile([P, S], U8, name="z_scales", align_bytes=64)
+        hs = [sb.tile([P, S], F32, name=f"h{t}") for t in range(PACK)]
+        for h in range(2):
+            nc.vector.tensor_copy(z_grouped[h][:], z_flat[:, h * 2 * S : (h + 1) * 2 * S].bitcast(I32).rearrange("p (u j) -> p j u", u=2))
+        for h in range(2):
+            quantize(z_codes[:, cols(h)], z_scales[:, cols(h)], z_grouped[h][:].rearrange("p j u -> p (j u)").bitcast(BF16))
+            product(h_banks[0][h], w2_codes, w2_scales, 0, z_codes[:, cols(h)], z_scales[:, cols(h)])
+            nc.scalar.activation(hs[0][:, cols(h)], h_banks[0][h], COPY, scale=0.75)
+        for t in range(1, PACK):
+            product(h_banks[t][:], w2_codes, w2_scales, t, z_codes[:], z_scales[:])
+
+        left = [sb.tile([P, S], F32, name=f"left{t}") for t in range(PACK)]
+        right = [sb.tile([P, S], F32, name=f"right{t}") for t in range(PACK)]
+        res = [sb.tile([P, S], F32, name=f"res{t}") for t in range(PACK)]
+        out_rows = out.rearrange("(p t) j -> p t j", t=PACK)
+
+        def make_left(t, h):
+            nc.vector.tensor_tensor(left[t][:, cols(h)], y[t][:].indirect(entries(n4_t, h)), hs[t][:, cols(h)], MULT)
+
+        def make_right(t, h):
+            nc.vector.tensor_tensor(right[t][:, cols(h)], hs[t][:].indirect(entries(n3_t, h)), y[t][:, cols(h)], MULT)
+
+        def finish(t, c):
+            nc.vector.tensor_tensor(res[t][:, c], left[t][:, c], right[t][:, c], SUB)
+            nc.sync.dma_start(out_rows[:, t, c], res[t][:, c])
+
+        for t in range(PACK):
+            if t > 0:
+                empty(y[t], y_banks, t, 1.0)
+                empty(hs[t], h_banks, t, 0.75)
+            make_left(t, 0)
+            if t > 0:
+                finish(t - 1, slice(0, S))
+            if t < PACK - 1:
+                make_left(t, 1)
+                make_right(t, 0)
+                make_right(t, 1)
+        last = PACK - 1
+        make_right(last, 0)
+        make_left(last, 1)
+        finish(last, cols(0))
+        make_right(last, 1)
+        finish(last, cols(1))

@@ -1,6 +1,7 @@
 from contextlib import ExitStack
 
 import concourse.mybir as mybir
+from concourse.masks import make_identity
 
 K, T, S, H, N, W = 512, 2048, 512, 512, 512, 256
 FLOPS = 2 * K * H * S + 2 * H * N * S
@@ -21,6 +22,8 @@ P = 128
 PACK = 4
 HALF = S // 2
 PER_COL = 16
+SUMMED = 3
+SCALAR_SHARE = 20
 
 
 def tile_picked_skipcrossbfold_none_p_kernel(tc, x_words, x_scales, w1, gn, w2, offs, n1, n2, n3, n4, out):
@@ -33,8 +36,8 @@ def tile_picked_skipcrossbfold_none_p_kernel(tc, x_words, x_scales, w1, gn, w2, 
         def cols(h):
             return slice(h * HALF, (h + 1) * HALF)
 
-        def entries(lst, h):
-            return lst[:, h * HALF // PER_COL : (h + 1) * HALF // PER_COL]
+        def entries(lst, c):
+            return lst[:, c.start // PER_COL : c.stop // PER_COL]
 
         warm = sb.tile([P, 2], F32, name="warm")
         nc.vector.memset(warm[:, 0:1], 0.0)
@@ -56,9 +59,9 @@ def tile_picked_skipcrossbfold_none_p_kernel(tc, x_words, x_scales, w1, gn, w2, 
         for q in range(4):
             nc.sync.dma_start(scale_table[32 * q : 32 * q + 4, :].bitcast(I32), x_scales[0, 4 * q : 4 * q + 4, :].bitcast(I32))
         offs_t = load_list(offs, "offs_t")
-        w1_raw.append(load_half(w1, 1))
         word_table = sb.tile([P, T], I32, name="word_table")
         nc.sync.dma_start(word_table[:], x_words[0].rearrange("p n r -> p (n r)").bitcast(I32))
+        w1_raw.append(load_half(w1, 1))
         n2_t = load_list(n2, "n2_t")
         n1_t = load_list(n1, "n1_t")
         gain = sb.tile([P, PACK], F32, name="gain")
@@ -66,9 +69,12 @@ def tile_picked_skipcrossbfold_none_p_kernel(tc, x_words, x_scales, w1, gn, w2, 
         n4_t = load_list(n4, "n4_t")
         n3_t = load_list(n3, "n3_t")
 
-        def deal(copy, grouped, m0, raw):
-            count = raw.shape[2] // PACK
-            copy(grouped[:, :, m0 : m0 + count, :].rearrange("p t m j -> p m j t"), raw.rearrange("p j (m t) -> p m j t", t=PACK))
+        ident = sb.tile([P, P], F32, name="ident")
+        make_identity(nc, ident[:])
+
+        def deal(copy, grouped, h, raw, tiles, m0=0, m1=P // 2):
+            m = slice(h * P // 2 + m0, h * P // 2 + m1)
+            copy(grouped[:, tiles, m, :].rearrange("p t m j -> p m j t"), raw[:].rearrange("p j (m t) -> p m j t", t=PACK)[:, m0:m1, :, tiles])
 
         def quantize(codes, scales, values):
             nc.vector.quantize_mx(out=codes.bitcast(FP8X4), scales=scales, in_=values)
@@ -82,11 +88,14 @@ def tile_picked_skipcrossbfold_none_p_kernel(tc, x_words, x_scales, w1, gn, w2, 
         x_bytes = sb.tile([P, S], U8, name="x_bytes", align_bytes=64)
         nc.vector.tensor_copy(x_bytes[:], scale_table[:].indirect(offs_t[:]))
         w1_grouped = sb.tile([P, PACK, P, PACK], BF16, name="w1_grouped", align_bytes=64)
-        deal(nc.scalar.copy, w1_grouped, 0, w1_raw[0][:])
-        deal(nc.vector.tensor_copy, w1_grouped, P // 2, w1_raw[1][:])
+        deal(nc.scalar.copy, w1_grouped, 0, w1_raw[0], slice(0, PACK))
+        nc.vector.tensor_copy(x_codes[:], word_table[:].bitcast(U32).indirect(offs_t[:]))
+        deal(nc.scalar.copy, w1_grouped, 1, w1_raw[1], slice(0, PACK), 0, SCALAR_SHARE)
+        deal(nc.vector.tensor_copy, w1_grouped, 1, w1_raw[1], slice(0, PACK), SCALAR_SHARE, P // 2)
         w1_codes = sb.tile([P, H], U32, name="w1_codes", align_bytes=64)
         w1_scales = sb.tile([P, H], U8, name="w1_scales", align_bytes=64)
-        quantize(w1_codes[:], w1_scales[:], w1_grouped[:].rearrange("p t m j -> p (t m j)"))
+        for t0, t1 in ((0, 1), (1, 2), (2, 4)):
+            quantize(w1_codes[:, t0 * P : t1 * P], w1_scales[:, t0 * P : t1 * P], w1_grouped[:, t0:t1, :, :].rearrange("p t m j -> p (t m j)"))
 
         w2_raw = [load_half(w2, h) for h in range(2)]
 
@@ -97,7 +106,6 @@ def tile_picked_skipcrossbfold_none_p_kernel(tc, x_words, x_scales, w1, gn, w2, 
         ds = [sb.tile([P, S], F32, name=f"ds{t}") for t in range(PACK)]
         y = [sb.tile([P, S], F32, name=f"y{t}") for t in range(PACK)]
         for h in range(2):
-            nc.vector.tensor_copy(x_codes[:, cols(h)], word_table[:].bitcast(U32).indirect(entries(offs_t, h)))
             product(y_banks[0][h], w1_codes, w1_scales, 0, x_codes[:, cols(h)], x_bytes[:, cols(h)])
             nc.scalar.copy(ds[0][:, cols(h)], y_banks[0][h])
         for t in range(1, PACK):
@@ -121,8 +129,10 @@ def tile_picked_skipcrossbfold_none_p_kernel(tc, x_words, x_scales, w1, gn, w2, 
         def fetch(t):
             if t > 0:
                 empty(ds[t], y_banks, t, 1.0)
-            nc.scalar.activation(gate[t][:], ds[t][:].indirect(n2_t[:]), SIGMOID)
             nc.vector.tensor_copy(pa[t][:], ds[t][:].indirect(n1_t[:]))
+
+        def make_gate(t):
+            nc.scalar.activation(gate[t][:], ds[t][:].indirect(n2_t[:]), SIGMOID)
 
         def put(t):
             nc.vector.tensor_tensor(ds[t][:].indirect(n2_t[:]), pa[t][:], gate[t][:], MULT)
@@ -134,27 +144,35 @@ def tile_picked_skipcrossbfold_none_p_kernel(tc, x_words, x_scales, w1, gn, w2, 
                 for h in range(2):
                     nc.scalar.activation(z_pairs[:, h, t // 2, :, t % 2], ds[t][:, cols(h)], COPY, scale=gain[:, t : t + 1])
 
-        def deal_w2(q):
-            deal(nc.scalar.copy, w2_grouped, q * 32, w2_raw[q // 2][:, :, (q % 2) * P : (q % 2 + 1) * P])
+        def deal_w2(u, h):
+            deal(nc.scalar.copy, w2_grouped, h, w2_raw[h], slice(2 * u, 2 * u + 2))
 
+        def quantize_w2(u):
+            quantize(w2_codes[:, cols(u)], w2_scales[:, cols(u)], w2_grouped[:, 2 * u : 2 * u + 2, :, :].rearrange("p t m j -> p (t m j)"))
+
+        neg_y = [sb.tile([P, S], F32, name=f"neg_y{t}") for t in range(SUMMED)]
         fetch(0)
+        make_gate(0)
         put(0)
         fetch(1)
         fetch(2)
-        cast(0)
+        make_gate(1)
         put(1)
         fetch(3)
-        deal_w2(0)
+        make_gate(2)
+        cast(0)
+        make_gate(3)
         cast(1)
-        deal_w2(1)
+        deal_w2(0, 0)
+        deal_w2(0, 1)
         put(2)
-        deal_w2(2)
         cast(2)
-        deal_w2(3)
+        deal_w2(1, 0)
         put(3)
+        quantize_w2(0)
         cast(3)
         empty(y[0], y_banks, 0, 1.0)
-        quantize(w2_codes[:], w2_scales[:], w2_grouped[:].rearrange("p t m j -> p (t m j)"))
+        empty(neg_y[0], y_banks, 0, -1.0)
 
         z_grouped = [sb.tile([P, HALF, 2], I32, name=f"z_grouped{h}", align_bytes=64) for h in range(2)]
         z_codes = sb.tile([P, S], U32, name="z_codes", align_bytes=64)
@@ -166,6 +184,11 @@ def tile_picked_skipcrossbfold_none_p_kernel(tc, x_words, x_scales, w1, gn, w2, 
             quantize(z_codes[:, cols(h)], z_scales[:, cols(h)], z_grouped[h][:].rearrange("p j u -> p (j u)").bitcast(BF16))
             product(h_banks[0][h], w2_codes, w2_scales, 0, z_codes[:, cols(h)], z_scales[:, cols(h)])
             nc.scalar.activation(hs[0][:, cols(h)], h_banks[0][h], COPY, scale=0.75)
+        y0_picked = sb.tile([P, S], F32, name="y0_picked")
+        for h in range(2):
+            nc.vector.tensor_copy(y0_picked[:, cols(h)], y[0][:].indirect(entries(n4_t, cols(h))))
+        deal_w2(1, 1)
+        quantize_w2(1)
         for t in range(1, PACK):
             product(h_banks[t][:], w2_codes, w2_scales, t, z_codes[:], z_scales[:])
 
@@ -174,30 +197,70 @@ def tile_picked_skipcrossbfold_none_p_kernel(tc, x_words, x_scales, w1, gn, w2, 
         res = [sb.tile([P, S], F32, name=f"res{t}") for t in range(PACK)]
         out_rows = out.rearrange("(p t) j -> p t j", t=PACK)
 
-        def make_left(t, h):
-            nc.vector.tensor_tensor(left[t][:, cols(h)], y[t][:].indirect(entries(n4_t, h)), hs[t][:, cols(h)], MULT)
+        def make_left(t, c):
+            nc.vector.tensor_tensor(left[t][:, c], y[t][:].indirect(entries(n4_t, c)), hs[t][:, c], MULT)
 
-        def make_right(t, h):
-            nc.vector.tensor_tensor(right[t][:, cols(h)], hs[t][:].indirect(entries(n3_t, h)), y[t][:, cols(h)], MULT)
+        def make_right(t, c):
+            factor = neg_y[t] if t < SUMMED else y[t]
+            nc.vector.tensor_tensor(right[t][:, c], hs[t][:].indirect(entries(n3_t, c)), factor[:, c], MULT)
 
         def finish(t, c):
             nc.vector.tensor_tensor(res[t][:, c], left[t][:, c], right[t][:, c], SUB)
             nc.sync.dma_start(out_rows[:, t, c], res[t][:, c])
 
-        for t in range(PACK):
-            if t > 0:
-                empty(y[t], y_banks, t, 1.0)
-                empty(hs[t], h_banks, t, 0.75)
-            make_left(t, 0)
-            if t > 0:
-                finish(t - 1, slice(0, S))
-            if t < PACK - 1:
-                make_left(t, 1)
-                make_right(t, 0)
-                make_right(t, 1)
+        turned = [sb.tile([P, S], F32, name=f"turned{t}") for t in range(SUMMED)]
+        def add_turned(t, c, tag):
+            acc = ps.tile([P, c.stop - c.start], F32, name="acc", tag=tag)
+            for b in range(c.start, c.stop, P):
+                blk = slice(b, b + P)
+                dst = acc[:, b - c.start : b - c.start + P]
+                nc.tensor.matmul(dst, left[t][:, blk], ident[:], start=True, stop=False, is_transpose=True)
+                nc.tensor.matmul(dst, right[t][:, blk], ident[:], start=False, stop=True, is_transpose=True)
+            nc.scalar.copy(turned[t][:, c], acc[:])
+
+        def turn_back(t, c, tag):
+            back = ps.tile([P, c.stop - c.start], F32, name="back", tag=tag)
+            for b in range(c.start, c.stop, P):
+                nc.tensor.transpose(back[:, b - c.start : b - c.start + P], turned[t][:, b : b + P], ident[:])
+            nc.scalar.copy(res[t][:, c], back[:])
+            nc.scalar.dma_start(out_rows[:, t, c], res[t][:, c])
+
+        def bring(t):
+            empty(y[t], y_banks, t, 1.0)
+            empty(hs[t], h_banks, t, 0.75)
+            if t < SUMMED:
+                empty(neg_y[t], y_banks, t, -1.0)
+
+        def add_up(t):
+            for h in range(2):
+                add_turned(t, cols(h), ("shared0", "y_bank1")[h])
+            for h in range(2):
+                turn_back(t, cols(h), ("shared1", "h_bank1")[h])
+
+        for h in range(2):
+            nc.vector.tensor_tensor(left[0][:, cols(h)], y0_picked[:, cols(h)], hs[0][:, cols(h)], MULT)
+        for h in range(2):
+            make_right(0, cols(h))
+        bring(1)
+        for h in range(2):
+            make_left(1, cols(h))
+        for h in range(2):
+            make_right(1, cols(h))
+        empty(y[2], y_banks, 2, 1.0)
+        empty(neg_y[2], y_banks, 2, -1.0)
+        empty(hs[2], h_banks, 2, 0.75)
+        bring(3)
+        add_up(0)
+        for h in range(2):
+            make_left(2, cols(h))
+            make_right(2, cols(h))
+        add_up(1)
+        add_up(2)
         last = PACK - 1
-        make_right(last, 0)
-        make_left(last, 1)
-        finish(last, cols(0))
-        make_right(last, 1)
-        finish(last, cols(1))
+        wide, narrow = slice(0, S - P), slice(S - P, S)
+        make_left(last, wide)
+        make_right(last, wide)
+        make_left(last, narrow)
+        finish(last, wide)
+        make_right(last, narrow)
+        finish(last, narrow)

@@ -54,7 +54,7 @@ def tile_picked_skipcrossbfold_none_p_kernel(tc, x_words, x_scales, w1, gn, w2, 
             return lst
 
         scale_table = sb.tile([P, T], U8, name="scale_table")
-        nc.vector.memset(scale_table[:].bitcast(I32), 0)
+        nc.gpsimd.memset(scale_table[:].bitcast(I32), 0)
         w1_raw = [load_half(w1, 0)]
         for q in range(4):
             nc.sync.dma_start(scale_table[32 * q : 32 * q + 4, :].bitcast(I32), x_scales[0, 4 * q : 4 * q + 4, :].bitcast(I32))
@@ -104,7 +104,8 @@ def tile_picked_skipcrossbfold_none_p_kernel(tc, x_words, x_scales, w1, gn, w2, 
         h_banks = [[shared[h][:, cols(1)] for h in range(2)]] + [ps.tile([P, S], F32, name=f"h_bank{t}") for t in range(1, PACK)]
 
         ds = [sb.tile([P, S], F32, name=f"ds{t}") for t in range(PACK)]
-        y = [sb.tile([P, S], F32, name=f"y{t}") for t in range(PACK)]
+        y_tile = [sb.tile([P, 2 * S], F32, name=f"y_tile{t}") for t in range(PACK)]
+        y = [tile[:, 0:S] for tile in y_tile]
         for h in range(2):
             product(y_banks[0][h], w1_codes, w1_scales, 0, x_codes[:, cols(h)], x_bytes[:, cols(h)])
             nc.scalar.copy(ds[0][:, cols(h)], y_banks[0][h])
@@ -116,26 +117,25 @@ def tile_picked_skipcrossbfold_none_p_kernel(tc, x_words, x_scales, w1, gn, w2, 
                 for h in range(2):
                     nc.scalar.activation(dst[:, cols(h)], banks[0][h], COPY, scale=scale)
             else:
-                nc.scalar.activation(dst[:], banks[t][:], COPY, scale=scale)
+                nc.scalar.activation(dst[:, 0:S], banks[t][:], COPY, scale=scale)
 
-        gate = [sb.tile([P, W], F32, name=f"gate{t}") for t in range(PACK)]
-        pa = [sb.tile([P, W], F32, name=f"pa{t}") for t in range(PACK)]
+        pa = [tile[:, S : S + W] for tile in y_tile[:3]] + [sb.tile([P, W], F32, name="pa3", align_bytes=64)[:]]
+        gate = [tile[:, S + W : 2 * S] for tile in y_tile[:3]] + [sb.tile([P, W], F32, name="gate3", align_bytes=64)[:]]
         z_flat = sb.tile([P, PACK * S], BF16, name="z_flat")
         z_pairs = z_flat[:].rearrange("p (h u j e) -> p h u j e", h=2, u=2, e=2)
-        w2_grouped = sb.tile([P, PACK, P, PACK], BF16, name="w2_grouped", align_bytes=64)
-        w2_codes = sb.tile([P, N], U32, name="w2_codes", align_bytes=64)
-        w2_scales = sb.tile([P, N], U8, name="w2_scales", align_bytes=64)
 
         def fetch(t):
             if t > 0:
                 empty(ds[t], y_banks, t, 1.0)
-            nc.vector.tensor_copy(pa[t][:], ds[t][:].indirect(n1_t[:]))
+            if t >= 2:
+                nc.sync.dma_start(y[t], ds[t][:])
+            nc.vector.tensor_copy(pa[t], ds[t][:].indirect(n1_t[:]))
 
         def make_gate(t):
-            nc.scalar.activation(gate[t][:], ds[t][:].indirect(n2_t[:]), SIGMOID)
+            nc.scalar.activation(gate[t], ds[t][:].indirect(n2_t[:]), SIGMOID)
 
         def put(t):
-            nc.vector.tensor_tensor(ds[t][:].indirect(n2_t[:]), pa[t][:], gate[t][:], MULT)
+            nc.vector.tensor_tensor(ds[t][:].indirect(n2_t[:]), pa[t], gate[t], MULT)
 
         def cast(t):
             if t < PACK - 1:
@@ -144,11 +144,17 @@ def tile_picked_skipcrossbfold_none_p_kernel(tc, x_words, x_scales, w1, gn, w2, 
                 for h in range(2):
                     nc.scalar.activation(z_pairs[:, h, t // 2, :, t % 2], ds[t][:, cols(h)], COPY, scale=gain[:, t : t + 1])
 
-        def deal_w2(u, h):
-            deal(nc.scalar.copy, w2_grouped, h, w2_raw[h], slice(2 * u, 2 * u + 2))
+        def deal_w2(grouped, u):
+            for h in range(2):
+                m = slice(h * P // 2, (h + 1) * P // 2)
+                nc.scalar.copy(grouped[:, :, m, :].rearrange("p t m j -> p m j t"),
+                               w2_raw[h][:].rearrange("p j (m t) -> p m j t", t=PACK)[:, :, :, 2 * u : 2 * u + 2])
 
-        def quantize_w2(u):
-            quantize(w2_codes[:, cols(u)], w2_scales[:, cols(u)], w2_grouped[:, 2 * u : 2 * u + 2, :, :].rearrange("p t m j -> p (t m j)"))
+        def quantize_w2(grouped, tag):
+            codes = sb.tile([P, 2 * P], U32, name="codes", tag=tag, align_bytes=64)
+            scales = sb.tile([P, 2 * P], U8, name="scales", tag=tag + "_scales", align_bytes=64)
+            quantize(codes[:], scales[:], grouped[:].rearrange("p t m j -> p (t m j)"))
+            return codes, scales
 
         neg_y = [sb.tile([P, S], F32, name=f"neg_y{t}") for t in range(SUMMED)]
         fetch(0)
@@ -163,13 +169,12 @@ def tile_picked_skipcrossbfold_none_p_kernel(tc, x_words, x_scales, w1, gn, w2, 
         cast(0)
         make_gate(3)
         cast(1)
-        deal_w2(0, 0)
-        deal_w2(0, 1)
+        w2_low = sb.tile([P, 2, P, PACK], BF16, name="w2_low", align_bytes=64)
+        deal_w2(w2_low, 0)
         put(2)
         cast(2)
-        deal_w2(1, 0)
         put(3)
-        quantize_w2(0)
+        low_codes, low_scales = quantize_w2(w2_low, "pa3")
         cast(3)
         empty(y[0], y_banks, 0, 1.0)
         empty(neg_y[0], y_banks, 0, -1.0)
@@ -177,32 +182,34 @@ def tile_picked_skipcrossbfold_none_p_kernel(tc, x_words, x_scales, w1, gn, w2, 
         z_grouped = [sb.tile([P, HALF, 2], I32, name=f"z_grouped{h}", align_bytes=64) for h in range(2)]
         z_codes = sb.tile([P, S], U32, name="z_codes", align_bytes=64)
         z_scales = sb.tile([P, S], U8, name="z_scales", align_bytes=64)
-        hs = [sb.tile([P, S], F32, name=f"h{t}") for t in range(PACK)]
+        h_tile = [sb.tile([P, 2 * S], F32, name=f"h_tile{t}") for t in range(3)] + [sb.tile([P, S], F32, name="h_tile3")]
+        hs = [tile[:, 0:S] for tile in h_tile]
         for h in range(2):
             nc.vector.tensor_copy(z_grouped[h][:], z_flat[:, h * 2 * S : (h + 1) * 2 * S].bitcast(I32).rearrange("p (u j) -> p j u", u=2))
         for h in range(2):
             quantize(z_codes[:, cols(h)], z_scales[:, cols(h)], z_grouped[h][:].rearrange("p j u -> p (j u)").bitcast(BF16))
-            product(h_banks[0][h], w2_codes, w2_scales, 0, z_codes[:, cols(h)], z_scales[:, cols(h)])
+            product(h_banks[0][h], low_codes, low_scales, 0, z_codes[:, cols(h)], z_scales[:, cols(h)])
             nc.scalar.activation(hs[0][:, cols(h)], h_banks[0][h], COPY, scale=0.75)
-        y0_picked = sb.tile([P, S], F32, name="y0_picked")
-        for h in range(2):
-            nc.vector.tensor_copy(y0_picked[:, cols(h)], y[0][:].indirect(entries(n4_t, cols(h))))
-        deal_w2(1, 1)
-        quantize_w2(1)
-        for t in range(1, PACK):
-            product(h_banks[t][:], w2_codes, w2_scales, t, z_codes[:], z_scales[:])
+        y0_picked = h_tile[0][:, S : 2 * S]
+        nc.vector.tensor_copy(y0_picked, y_tile[0][:].indirect(n4_t[:]))
+        product(h_banks[1][:], low_codes, low_scales, 1, z_codes[:], z_scales[:])
+        w2_high = sb.tile([P, 2, P, PACK], BF16, name="w2_high", tag="gate3", align_bytes=64)
+        deal_w2(w2_high, 1)
+        high_codes, high_scales = quantize_w2(w2_high, "w2_high_codes")
+        for t in range(2, PACK):
+            product(h_banks[t][:], high_codes, high_scales, t - 2, z_codes[:], z_scales[:])
 
-        left = [sb.tile([P, S], F32, name=f"left{t}") for t in range(PACK)]
-        right = [sb.tile([P, S], F32, name=f"right{t}") for t in range(PACK)]
+        left = [h_tile[t + 1][:, S : 2 * S] for t in range(2)] + [sb.tile([P, S], F32, name=f"left{t}")[:] for t in range(2, PACK)]
+        right = [y_tile[3][:, S : 2 * S]] + [sb.tile([P, S], F32, name=f"right{t}")[:] for t in range(1, PACK)]
         res = [sb.tile([P, S], F32, name=f"res{t}") for t in range(PACK)]
         out_rows = out.rearrange("(p t) j -> p t j", t=PACK)
 
         def make_left(t, c):
-            nc.vector.tensor_tensor(left[t][:, c], y[t][:].indirect(entries(n4_t, c)), hs[t][:, c], MULT)
+            nc.vector.tensor_tensor(left[t][:, c], y_tile[t][:].indirect(entries(n4_t, c)), hs[t][:, c], MULT)
 
         def make_right(t, c):
             factor = neg_y[t] if t < SUMMED else y[t]
-            nc.vector.tensor_tensor(right[t][:, c], hs[t][:].indirect(entries(n3_t, c)), factor[:, c], MULT)
+            nc.vector.tensor_tensor(right[t][:, c], h_tile[t][:].indirect(entries(n3_t, c)), factor[:, c], MULT)
 
         def finish(t, c):
             nc.vector.tensor_tensor(res[t][:, c], left[t][:, c], right[t][:, c], SUB)
@@ -225,42 +232,32 @@ def tile_picked_skipcrossbfold_none_p_kernel(tc, x_words, x_scales, w1, gn, w2, 
             nc.scalar.copy(res[t][:, c], back[:])
             nc.scalar.dma_start(out_rows[:, t, c], res[t][:, c])
 
-        def bring(t):
-            empty(y[t], y_banks, t, 1.0)
-            empty(hs[t], h_banks, t, 0.75)
-            if t < SUMMED:
-                empty(neg_y[t], y_banks, t, -1.0)
-
         def add_up(t):
             for h in range(2):
                 add_turned(t, cols(h), ("shared0", "y_bank1")[h])
             for h in range(2):
                 turn_back(t, cols(h), ("shared1", "h_bank1")[h])
 
-        for h in range(2):
-            nc.vector.tensor_tensor(left[0][:, cols(h)], y0_picked[:, cols(h)], hs[0][:, cols(h)], MULT)
-        for h in range(2):
-            make_right(0, cols(h))
-        bring(1)
-        for h in range(2):
-            make_left(1, cols(h))
-        for h in range(2):
-            make_right(1, cols(h))
-        empty(y[2], y_banks, 2, 1.0)
-        empty(neg_y[2], y_banks, 2, -1.0)
+        whole = slice(0, S)
+        nc.vector.tensor_tensor(left[0], y0_picked, hs[0], MULT)
+        make_right(0, whole)
+        empty(y[1], y_banks, 1, 1.0)
+        empty(hs[1], h_banks, 1, 0.75)
+        empty(neg_y[1], y_banks, 1, -1.0)
+        make_left(1, whole)
+        make_right(1, whole)
         empty(hs[2], h_banks, 2, 0.75)
-        bring(3)
+        empty(neg_y[2], y_banks, 2, -1.0)
+        empty(hs[3], h_banks, 3, 0.75)
         add_up(0)
-        for h in range(2):
-            make_left(2, cols(h))
-            make_right(2, cols(h))
+        make_left(2, whole)
+        make_right(2, whole)
         add_up(1)
         add_up(2)
         last = PACK - 1
         wide, narrow = slice(0, S - P), slice(S - P, S)
-        make_left(last, wide)
+        make_left(last, whole)
         make_right(last, wide)
-        make_left(last, narrow)
-        finish(last, wide)
         make_right(last, narrow)
+        finish(last, wide)
         finish(last, narrow)

@@ -22,7 +22,7 @@ P = 128
 PACK = 4
 HALF = S // 2
 PER_COL = 16
-SUMMED = 3
+SUMMED = 2
 SCALAR_SHARE = 20
 
 
@@ -247,16 +247,15 @@ def tile_picked_skipcrossbfold_none_p_kernel(tc, x_words, x_scales, w1, gn, w2, 
         make_left(1, whole)
         make_right(1, whole)
         empty(hs[2], h_banks, 2, 0.75)
-        empty(neg_y[2], y_banks, 2, -1.0)
         empty(hs[3], h_banks, 3, 0.75)
         add_up(0)
         make_left(2, whole)
         make_right(2, whole)
         add_up(1)
-        add_up(2)
         last = PACK - 1
         wide, narrow = slice(0, S - P), slice(S - P, S)
         make_left(last, whole)
+        finish(2, whole)
         make_right(last, wide)
         make_right(last, narrow)
         finish(last, wide)

@@ -21,9 +21,20 @@ SIGMOID = mybir.ActivationFunctionType.Sigmoid
 P = 128
 PACK = 4
 HALF = S // 2
-PER_COL = 16
-SUMMED = 2
-SCALAR_SHARE = 20
+PER_COLUMN = 16
+MX_ALIGN = 64
+OUT_SCALE = 0.75
+SCALAR_GROUPS = 20
+WHOLE = slice(0, S)
+SPARE = slice(S, 2 * S)
+
+
+def half(h):
+    return slice(h * HALF, (h + 1) * HALF)
+
+
+def entries(lst, c):
+    return lst[:, c.start // PER_COLUMN : c.stop // PER_COLUMN]
 
 
 def tile_picked_skipcrossbfold_none_p_kernel(tc, x_words, x_scales, w1, gn, w2, offs, n1, n2, n3, n4, out):
@@ -33,19 +44,13 @@ def tile_picked_skipcrossbfold_none_p_kernel(tc, x_words, x_scales, w1, gn, w2, 
         sb = ctx.enter_context(tc.tile_pool(name="sb", bufs=1))
         ps = ctx.enter_context(tc.psum_pool(name="ps", bufs=1))
 
-        def cols(h):
-            return slice(h * HALF, (h + 1) * HALF)
-
-        def entries(lst, c):
-            return lst[:, c.start // PER_COL : c.stop // PER_COL]
-
         warm = sb.tile([P, 2], F32, name="warm")
         nc.vector.memset(warm[:, 0:1], 0.0)
         nc.scalar.activation(warm[:, 1:2], warm[:, 0:1], SIGMOID)
 
         def load_half(w, h):
             raw = sb.tile([P, PACK, HALF], F32, name="raw", tag=f"raw{h}")
-            nc.sync.dma_start(raw[:], w.rearrange("(p j) c -> p j c", j=PACK)[:, :, cols(h)])
+            nc.sync.dma_start(raw[:], w.rearrange("(p j) c -> p j c", j=PACK)[:, :, half(h)])
             return raw
 
         def load_list(src, name):
@@ -72,61 +77,61 @@ def tile_picked_skipcrossbfold_none_p_kernel(tc, x_words, x_scales, w1, gn, w2, 
         ident = sb.tile([P, P], F32, name="ident")
         make_identity(nc, ident[:])
 
-        def deal(copy, grouped, h, raw, tiles, m0=0, m1=P // 2):
+        def deal(copy, grouped, raw, h, tiles, m0, m1):
             m = slice(h * P // 2 + m0, h * P // 2 + m1)
-            copy(grouped[:, tiles, m, :].rearrange("p t m j -> p m j t"), raw[:].rearrange("p j (m t) -> p m j t", t=PACK)[:, m0:m1, :, tiles])
+            copy(grouped[:, :, m, :].rearrange("p t m j -> p m j t"), raw[:].rearrange("p j (m t) -> p m j t", t=PACK)[:, m0:m1, :, tiles])
 
         def quantize(codes, scales, values):
             nc.vector.quantize_mx(out=codes.bitcast(FP8X4), scales=scales, in_=values)
 
-        def product(acc, w_codes, w_scales, t, codes, scales):
-            m = slice(t * P, (t + 1) * P)
+        def product(acc, w_codes, w_scales, slot, codes, scales):
+            m = slice(slot * P, (slot + 1) * P)
             nc.tensor.matmul_mx(out=acc, lhsT=w_codes[:, m].bitcast(FP8X4), lhsT_scale=w_scales[:, m],
                                 rhs=codes.bitcast(FP8X4), rhs_scale=scales, start=True, stop=True)
 
-        x_codes = sb.tile([P, S], U32, name="x_codes", align_bytes=64)
-        x_bytes = sb.tile([P, S], U8, name="x_bytes", align_bytes=64)
+        def empty(dst, banks, scale):
+            width = S // len(banks)
+            for i, bank in enumerate(banks):
+                nc.scalar.activation(dst[:, i * width : (i + 1) * width], bank, COPY, scale=scale)
+
+        x_codes = sb.tile([P, S], U32, name="x_codes", align_bytes=MX_ALIGN)
+        x_bytes = sb.tile([P, S], U8, name="x_bytes", align_bytes=MX_ALIGN)
         nc.vector.tensor_copy(x_bytes[:], scale_table[:].indirect(offs_t[:]))
-        w1_grouped = sb.tile([P, PACK, P, PACK], BF16, name="w1_grouped", align_bytes=64)
-        deal(nc.scalar.copy, w1_grouped, 0, w1_raw[0], slice(0, PACK))
+        w1_grouped = sb.tile([P, PACK, P, PACK], BF16, name="w1_grouped", align_bytes=MX_ALIGN)
+        all_tiles = slice(0, PACK)
+        deal(nc.scalar.copy, w1_grouped, w1_raw[0], 0, all_tiles, 0, P // 2)
         nc.vector.tensor_copy(x_codes[:], word_table[:].bitcast(U32).indirect(offs_t[:]))
-        deal(nc.scalar.copy, w1_grouped, 1, w1_raw[1], slice(0, PACK), 0, SCALAR_SHARE)
-        deal(nc.vector.tensor_copy, w1_grouped, 1, w1_raw[1], slice(0, PACK), SCALAR_SHARE, P // 2)
-        w1_codes = sb.tile([P, H], U32, name="w1_codes", align_bytes=64)
-        w1_scales = sb.tile([P, H], U8, name="w1_scales", align_bytes=64)
+        deal(nc.scalar.copy, w1_grouped, w1_raw[1], 1, all_tiles, 0, SCALAR_GROUPS)
+        deal(nc.vector.tensor_copy, w1_grouped, w1_raw[1], 1, all_tiles, SCALAR_GROUPS, P // 2)
+        w1_codes = sb.tile([P, H], U32, name="w1_codes", align_bytes=MX_ALIGN)
+        w1_scales = sb.tile([P, H], U8, name="w1_scales", align_bytes=MX_ALIGN)
         for t0, t1 in ((0, 1), (1, 2), (2, 4)):
             quantize(w1_codes[:, t0 * P : t1 * P], w1_scales[:, t0 * P : t1 * P], w1_grouped[:, t0:t1, :, :].rearrange("p t m j -> p (t m j)"))
 
         w2_raw = [load_half(w2, h) for h in range(2)]
 
-        shared = [ps.tile([P, S], F32, name=f"shared{h}") for h in range(2)]
-        y_banks = [[shared[h][:, cols(0)] for h in range(2)]] + [ps.tile([P, S], F32, name=f"y_bank{t}") for t in range(1, PACK)]
-        h_banks = [[shared[h][:, cols(1)] for h in range(2)]] + [ps.tile([P, S], F32, name=f"h_bank{t}") for t in range(1, PACK)]
+        split = [ps.tile([P, S], F32, name=f"split{h}") for h in range(2)]
+        y_banks = [[split[h][:, half(0)] for h in range(2)]] + [[ps.tile([P, S], F32, name=f"y_bank{t}")[:]] for t in (1, 2, 3)]
+        h_banks = {t: [ps.tile([P, S], F32, name=f"h_bank{t}")[:]] for t in (3, 0, 1)}
+        h_banks[2] = [split[h][:, half(1)] for h in range(2)]
 
         ds = [sb.tile([P, S], F32, name=f"ds{t}") for t in range(PACK)]
         y_tile = [sb.tile([P, 2 * S], F32, name=f"y_tile{t}") for t in range(PACK)]
-        y = [tile[:, 0:S] for tile in y_tile]
+        y = [tile[:, WHOLE] for tile in y_tile]
         for h in range(2):
-            product(y_banks[0][h], w1_codes, w1_scales, 0, x_codes[:, cols(h)], x_bytes[:, cols(h)])
-            nc.scalar.copy(ds[0][:, cols(h)], y_banks[0][h])
-        for t in range(1, PACK):
-            product(y_banks[t][:], w1_codes, w1_scales, t, x_codes[:], x_bytes[:])
+            product(y_banks[0][h], w1_codes, w1_scales, 0, x_codes[:, half(h)], x_bytes[:, half(h)])
+            nc.scalar.copy(ds[0][:, half(h)], y_banks[0][h])
+        for t in (1, 2, 3):
+            product(y_banks[t][0], w1_codes, w1_scales, t, x_codes[:], x_bytes[:])
 
-        def empty(dst, banks, t, scale):
-            if t == 0:
-                for h in range(2):
-                    nc.scalar.activation(dst[:, cols(h)], banks[0][h], COPY, scale=scale)
-            else:
-                nc.scalar.activation(dst[:, 0:S], banks[t][:], COPY, scale=scale)
-
-        pa = [tile[:, S : S + W] for tile in y_tile[:3]] + [sb.tile([P, W], F32, name="pa3", align_bytes=64)[:]]
-        gate = [tile[:, S + W : 2 * S] for tile in y_tile[:3]] + [sb.tile([P, W], F32, name="gate3", align_bytes=64)[:]]
+        pa = [tile[:, S : S + W] for tile in y_tile[:3]] + [sb.tile([P, W], F32, name="pa3", align_bytes=MX_ALIGN)[:]]
+        gate = [tile[:, S + W : 2 * S] for tile in y_tile[:3]] + [sb.tile([P, W], F32, name="gate3", align_bytes=MX_ALIGN)[:]]
         z_flat = sb.tile([P, PACK * S], BF16, name="z_flat")
         z_pairs = z_flat[:].rearrange("p (h u j e) -> p h u j e", h=2, u=2, e=2)
 
         def fetch(t):
             if t > 0:
-                empty(ds[t], y_banks, t, 1.0)
+                empty(ds[t], y_banks[t], 1.0)
             if t >= 2:
                 nc.sync.dma_start(y[t], ds[t][:])
             nc.vector.tensor_copy(pa[t], ds[t][:].indirect(n1_t[:]))
@@ -137,26 +142,22 @@ def tile_picked_skipcrossbfold_none_p_kernel(tc, x_words, x_scales, w1, gn, w2, 
         def put(t):
             nc.vector.tensor_tensor(ds[t][:].indirect(n2_t[:]), pa[t], gate[t], MULT)
 
-        def cast(t):
-            if t < PACK - 1:
-                nc.scalar.activation(z_pairs[:, :, t // 2, :, t % 2], ds[t][:].rearrange("p (h j) -> p h j", h=2), COPY, scale=gain[:, t : t + 1])
-            else:
-                for h in range(2):
-                    nc.scalar.activation(z_pairs[:, h, t // 2, :, t % 2], ds[t][:, cols(h)], COPY, scale=gain[:, t : t + 1])
+        def cast(t, halves):
+            nc.scalar.activation(z_pairs[:, halves, t // 2, :, t % 2], ds[t][:].rearrange("p (h j) -> p h j", h=2)[:, halves, :], COPY, scale=gain[:, t : t + 1])
 
-        def deal_w2(grouped, u):
+        def deal_w2(tiles, tag):
+            grouped = sb.tile([P, 2, P, PACK], BF16, name="grouped", tag=tag, align_bytes=MX_ALIGN)
             for h in range(2):
-                m = slice(h * P // 2, (h + 1) * P // 2)
-                nc.scalar.copy(grouped[:, :, m, :].rearrange("p t m j -> p m j t"),
-                               w2_raw[h][:].rearrange("p j (m t) -> p m j t", t=PACK)[:, :, :, 2 * u : 2 * u + 2])
+                deal(nc.scalar.copy, grouped, w2_raw[h], h, tiles, 0, P // 2)
+            return grouped
 
         def quantize_w2(grouped, tag):
-            codes = sb.tile([P, 2 * P], U32, name="codes", tag=tag, align_bytes=64)
-            scales = sb.tile([P, 2 * P], U8, name="scales", tag=tag + "_scales", align_bytes=64)
+            codes = sb.tile([P, 2 * P], U32, name="codes", tag=tag, align_bytes=MX_ALIGN)
+            scales = sb.tile([P, 2 * P], U8, name="scales", tag=tag + "_scales", align_bytes=MX_ALIGN)
             quantize(codes[:], scales[:], grouped[:].rearrange("p t m j -> p (t m j)"))
             return codes, scales
 
-        neg_y = [sb.tile([P, S], F32, name=f"neg_y{t}") for t in range(SUMMED)]
+        both = slice(0, 2)
         fetch(0)
         make_gate(0)
         put(0)
@@ -166,97 +167,99 @@ def tile_picked_skipcrossbfold_none_p_kernel(tc, x_words, x_scales, w1, gn, w2, 
         put(1)
         fetch(3)
         make_gate(2)
-        cast(0)
+        cast(0, both)
         make_gate(3)
-        cast(1)
-        w2_low = sb.tile([P, 2, P, PACK], BF16, name="w2_low", align_bytes=64)
-        deal_w2(w2_low, 0)
+        cast(1, both)
+        w2_early = deal_w2(slice(2, 4), "w2_early")
         put(2)
-        cast(2)
+        cast(2, both)
         put(3)
-        low_codes, low_scales = quantize_w2(w2_low, "pa3")
-        cast(3)
-        empty(y[0], y_banks, 0, 1.0)
-        empty(neg_y[0], y_banks, 0, -1.0)
-
-        z_grouped = [sb.tile([P, HALF, 2], I32, name=f"z_grouped{h}", align_bytes=64) for h in range(2)]
-        z_codes = sb.tile([P, S], U32, name="z_codes", align_bytes=64)
-        z_scales = sb.tile([P, S], U8, name="z_scales", align_bytes=64)
-        h_tile = [sb.tile([P, 2 * S], F32, name=f"h_tile{t}") for t in range(3)] + [sb.tile([P, S], F32, name="h_tile3")]
-        hs = [tile[:, 0:S] for tile in h_tile]
+        early_codes, early_scales = quantize_w2(w2_early, "pa3")
         for h in range(2):
-            nc.vector.tensor_copy(z_grouped[h][:], z_flat[:, h * 2 * S : (h + 1) * 2 * S].bitcast(I32).rearrange("p (u j) -> p j u", u=2))
-        for h in range(2):
-            quantize(z_codes[:, cols(h)], z_scales[:, cols(h)], z_grouped[h][:].rearrange("p j u -> p (j u)").bitcast(BF16))
-            product(h_banks[0][h], low_codes, low_scales, 0, z_codes[:, cols(h)], z_scales[:, cols(h)])
-            nc.scalar.activation(hs[0][:, cols(h)], h_banks[0][h], COPY, scale=0.75)
-        y0_picked = h_tile[0][:, S : 2 * S]
-        nc.vector.tensor_copy(y0_picked, y_tile[0][:].indirect(n4_t[:]))
-        product(h_banks[1][:], low_codes, low_scales, 1, z_codes[:], z_scales[:])
-        w2_high = sb.tile([P, 2, P, PACK], BF16, name="w2_high", tag="gate3", align_bytes=64)
-        deal_w2(w2_high, 1)
-        high_codes, high_scales = quantize_w2(w2_high, "w2_high_codes")
-        for t in range(2, PACK):
-            product(h_banks[t][:], high_codes, high_scales, t - 2, z_codes[:], z_scales[:])
+            cast(3, slice(h, h + 1))
+        w2_late = deal_w2(slice(0, 2), "gate3")
 
-        left = [h_tile[t + 1][:, S : 2 * S] for t in range(2)] + [sb.tile([P, S], F32, name=f"left{t}")[:] for t in range(2, PACK)]
-        right = [y_tile[3][:, S : 2 * S]] + [sb.tile([P, S], F32, name=f"right{t}")[:] for t in range(1, PACK)]
+        h_tile = [sb.tile([P, S if t == 1 else 2 * S], F32, name=f"h_tile{t}", align_bytes=MX_ALIGN) for t in range(PACK)]
+        hs = [tile[:, WHOLE] for tile in h_tile]
+        z_words = [h_tile[2][:, SPARE].bitcast(I32), sb.tile([P, S], I32, name="z_words1", align_bytes=MX_ALIGN)[:]]
+        z_codes = sb.tile([P, S], U32, name="z_codes", align_bytes=MX_ALIGN)
+        z_scales = sb.tile([P, S], U8, name="z_scales", align_bytes=MX_ALIGN)
+        for h in range(2):
+            pairs = z_flat[:, h * 2 * S : (h + 1) * 2 * S].bitcast(I32)
+            nc.vector.tensor_copy(z_words[h].rearrange("p (j u) -> p j u", u=2), pairs.rearrange("p (u j) -> p j u", u=2))
+        for h in range(2):
+            quantize(z_codes[:, half(h)], z_scales[:, half(h)], z_words[h].bitcast(BF16))
+            product(h_banks[2][h], early_codes, early_scales, 0, z_codes[:, half(h)], z_scales[:, half(h)])
+            nc.scalar.activation(hs[2][:, half(h)], h_banks[2][h], COPY, scale=OUT_SCALE)
+        y2_picked = h_tile[2][:, SPARE]
+        nc.vector.tensor_copy(y2_picked, y_tile[2][:].indirect(n4_t[:]))
+        product(h_banks[3][0], early_codes, early_scales, 1, z_codes[:], z_scales[:])
+        late_codes, late_scales = quantize_w2(w2_late, "late_codes")
+        for t in (0, 1):
+            product(h_banks[t][0], late_codes, late_scales, t, z_codes[:], z_scales[:])
+
+        left = {t: sb.tile([P, S], F32, name=f"left{t}")[:] for t in (0, 1)}
+        left[2], left[3] = y_tile[3][:, SPARE], h_tile[0][:, SPARE]
+        right = {t: sb.tile([P, S], F32, name=f"right{t}")[:] for t in (3, 0, 1)}
+        right[2] = h_tile[3][:, SPARE]
+        neg_y = {t: sb.tile([P, S], F32, name=f"neg_y{t}")[:] for t in (2, 3)}
+        turned = {t: sb.tile([P, S], F32, name=f"turned{t}") for t in (2, 3)}
         res = [sb.tile([P, S], F32, name=f"res{t}") for t in range(PACK)]
         out_rows = out.rearrange("(p t) j -> p t j", t=PACK)
 
-        def make_left(t, c):
-            nc.vector.tensor_tensor(left[t][:, c], y_tile[t][:].indirect(entries(n4_t, c)), hs[t][:, c], MULT)
+        def make_left(t):
+            nc.vector.tensor_tensor(left[t], y_tile[t][:].indirect(n4_t[:]), hs[t], MULT)
 
-        def make_right(t, c):
-            factor = neg_y[t] if t < SUMMED else y[t]
+        def make_right(t, c, factor):
             nc.vector.tensor_tensor(right[t][:, c], h_tile[t][:].indirect(entries(n3_t, c)), factor[:, c], MULT)
 
-        def finish(t, c):
+        def subtract(t, c):
             nc.vector.tensor_tensor(res[t][:, c], left[t][:, c], right[t][:, c], SUB)
             nc.sync.dma_start(out_rows[:, t, c], res[t][:, c])
 
-        turned = [sb.tile([P, S], F32, name=f"turned{t}") for t in range(SUMMED)]
-        def add_turned(t, c, tag):
-            acc = ps.tile([P, c.stop - c.start], F32, name="acc", tag=tag)
-            for b in range(c.start, c.stop, P):
-                blk = slice(b, b + P)
-                dst = acc[:, b - c.start : b - c.start + P]
-                nc.tensor.matmul(dst, left[t][:, blk], ident[:], start=True, stop=False, is_transpose=True)
-                nc.tensor.matmul(dst, right[t][:, blk], ident[:], start=False, stop=True, is_transpose=True)
-            nc.scalar.copy(turned[t][:, c], acc[:])
+        def add_turned(t, h):
+            acc = ps.tile([P, HALF], F32, name="acc", tag=("y_bank2", "y_bank3")[h])
+            for b in range(0, HALF, P):
+                block = slice(h * HALF + b, h * HALF + b + P)
+                nc.tensor.matmul(acc[:, b : b + P], left[t][:, block], ident[:], start=True, stop=False, is_transpose=True)
+                nc.tensor.matmul(acc[:, b : b + P], right[t][:, block], ident[:], start=False, stop=True, is_transpose=True)
+            nc.scalar.copy(turned[t][:, half(h)], acc[:])
 
-        def turn_back(t, c, tag):
-            back = ps.tile([P, c.stop - c.start], F32, name="back", tag=tag)
-            for b in range(c.start, c.stop, P):
-                nc.tensor.transpose(back[:, b - c.start : b - c.start + P], turned[t][:, b : b + P], ident[:])
-            nc.scalar.copy(res[t][:, c], back[:])
-            nc.scalar.dma_start(out_rows[:, t, c], res[t][:, c])
+        def turn_back(t, h):
+            back = ps.tile([P, HALF], F32, name="back", tag=("h_bank3", "split0")[h])
+            for b in range(0, HALF, P):
+                nc.tensor.transpose(back[:, b : b + P], turned[t][:, h * HALF + b : h * HALF + b + P], ident[:])
+            nc.scalar.copy(res[t][:, half(h)], back[:])
+            nc.scalar.dma_start(out_rows[:, t, half(h)], res[t][:, half(h)])
 
         def add_up(t):
             for h in range(2):
-                add_turned(t, cols(h), ("shared0", "y_bank1")[h])
+                add_turned(t, h)
             for h in range(2):
-                turn_back(t, cols(h), ("shared1", "h_bank1")[h])
+                turn_back(t, h)
 
-        whole = slice(0, S)
-        nc.vector.tensor_tensor(left[0], y0_picked, hs[0], MULT)
-        make_right(0, whole)
-        empty(y[1], y_banks, 1, 1.0)
-        empty(hs[1], h_banks, 1, 0.75)
-        empty(neg_y[1], y_banks, 1, -1.0)
-        make_left(1, whole)
-        make_right(1, whole)
-        empty(hs[2], h_banks, 2, 0.75)
-        empty(hs[3], h_banks, 3, 0.75)
-        add_up(0)
-        make_left(2, whole)
-        make_right(2, whole)
-        add_up(1)
-        last = PACK - 1
+        empty(neg_y[2], y_banks[2], -1.0)
+        nc.vector.tensor_tensor(left[2], y2_picked, hs[2], MULT)
+        make_right(2, WHOLE, neg_y[2])
+
+        empty(hs[3], h_banks[3], OUT_SCALE)
+        empty(neg_y[3], y_banks[3], -1.0)
+        make_left(3)
+        make_right(3, WHOLE, neg_y[3])
+
+        empty(y[0], y_banks[0], 1.0)
+        empty(hs[0], h_banks[0], OUT_SCALE)
+        empty(y[1], y_banks[1], 1.0)
+        empty(hs[1], h_banks[1], OUT_SCALE)
+        add_up(2)
+        make_left(0)
+        make_right(0, WHOLE, y[0])
+        add_up(3)
+
         wide, narrow = slice(0, S - P), slice(S - P, S)
-        make_left(last, whole)
-        finish(2, whole)
-        make_right(last, wide)
-        make_right(last, narrow)
-        finish(last, wide)
-        finish(last, narrow)
+        make_left(1)
+        subtract(0, WHOLE)
+        make_right(1, wide, y[1])
+        make_right(1, narrow, y[1])
+        subtract(1, wide)
+        subtract(1, narrow)

from contextlib import ExitStack

import concourse.mybir as mybir
from concourse.masks import make_identity

K, T, S, H, N, W = 512, 2048, 512, 512, 512, 256
FLOPS = 2 * K * H * S + 2 * H * N * S

F32 = mybir.dt.float32
BF16 = mybir.dt.bfloat16
I32 = mybir.dt.int32
U32 = mybir.dt.uint32
U16 = mybir.dt.uint16
U8 = mybir.dt.uint8
FP8X4 = mybir.dt.float8_e4m3fn_x4
MULT = mybir.AluOpType.mult
SUB = mybir.AluOpType.subtract
COPY = mybir.ActivationFunctionType.Copy
SIGMOID = mybir.ActivationFunctionType.Sigmoid

P = 128
PACK = 4
HALF = S // 2
PER_COLUMN = 16
MX_ALIGN = 64
OUT_SCALE = 0.75
SCALAR_GROUPS = 20
WHOLE = slice(0, S)
SPARE = slice(S, 2 * S)


def half(h):
    return slice(h * HALF, (h + 1) * HALF)


def entries(lst, c):
    return lst[:, c.start // PER_COLUMN : c.stop // PER_COLUMN]


def tile_picked_skipcrossbfold_none_p_kernel(tc, x_words, x_scales, w1, gn, w2, offs, n1, n2, n3, n4, out):
    nc = tc.nc
    with ExitStack() as ctx:
        lists = ctx.enter_context(tc.tile_pool(name="lists", bufs=1))
        sb = ctx.enter_context(tc.tile_pool(name="sb", bufs=1))
        ps = ctx.enter_context(tc.psum_pool(name="ps", bufs=1))

        warm = sb.tile([P, 2], F32, name="warm")
        nc.vector.memset(warm[:, 0:1], 0.0)
        nc.scalar.activation(warm[:, 1:2], warm[:, 0:1], SIGMOID)

        def load_half(w, h):
            raw = sb.tile([P, PACK, HALF], F32, name="raw", tag=f"raw{h}")
            nc.sync.dma_start(raw[:], w.rearrange("(p j) c -> p j c", j=PACK)[:, :, half(h)])
            return raw

        def load_list(src, name):
            lst = lists.tile(list(src.shape), U16, name=name)
            nc.sync.dma_start(lst[:], src)
            return lst

        scale_table = sb.tile([P, T], U8, name="scale_table")
        nc.gpsimd.memset(scale_table[:].bitcast(I32), 0)
        w1_raw = [load_half(w1, 0)]
        for q in range(4):
            nc.sync.dma_start(scale_table[32 * q : 32 * q + 4, :].bitcast(I32), x_scales[0, 4 * q : 4 * q + 4, :].bitcast(I32))
        offs_t = load_list(offs, "offs_t")
        word_table = sb.tile([P, T], I32, name="word_table")
        nc.sync.dma_start(word_table[:], x_words[0].rearrange("p n r -> p (n r)").bitcast(I32))
        w1_raw.append(load_half(w1, 1))
        n2_t = load_list(n2, "n2_t")
        n1_t = load_list(n1, "n1_t")
        gain = sb.tile([P, PACK], F32, name="gain")
        nc.sync.dma_start(gain[:], gn.rearrange("(p t) o -> p (t o)", t=PACK))
        n4_t = load_list(n4, "n4_t")
        n3_t = load_list(n3, "n3_t")

        ident = sb.tile([P, P], F32, name="ident")
        make_identity(nc, ident[:])

        def deal(copy, grouped, raw, h, tiles, m0, m1):
            m = slice(h * P // 2 + m0, h * P // 2 + m1)
            copy(grouped[:, :, m, :].rearrange("p t m j -> p m j t"), raw[:].rearrange("p j (m t) -> p m j t", t=PACK)[:, m0:m1, :, tiles])

        def quantize(codes, scales, values):
            nc.vector.quantize_mx(out=codes.bitcast(FP8X4), scales=scales, in_=values)

        def product(acc, w_codes, w_scales, slot, codes, scales):
            m = slice(slot * P, (slot + 1) * P)
            nc.tensor.matmul_mx(out=acc, lhsT=w_codes[:, m].bitcast(FP8X4), lhsT_scale=w_scales[:, m],
                                rhs=codes.bitcast(FP8X4), rhs_scale=scales, start=True, stop=True)

        def empty(dst, banks, scale):
            width = S // len(banks)
            for i, bank in enumerate(banks):
                nc.scalar.activation(dst[:, i * width : (i + 1) * width], bank, COPY, scale=scale)

        x_codes = sb.tile([P, S], U32, name="x_codes", align_bytes=MX_ALIGN)
        x_bytes = sb.tile([P, S], U8, name="x_bytes", align_bytes=MX_ALIGN)
        nc.vector.tensor_copy(x_bytes[:], scale_table[:].indirect(offs_t[:]))
        w1_grouped = sb.tile([P, PACK, P, PACK], BF16, name="w1_grouped", align_bytes=MX_ALIGN)
        all_tiles = slice(0, PACK)
        deal(nc.scalar.copy, w1_grouped, w1_raw[0], 0, all_tiles, 0, P // 2)
        nc.vector.tensor_copy(x_codes[:], word_table[:].bitcast(U32).indirect(offs_t[:]))
        deal(nc.scalar.copy, w1_grouped, w1_raw[1], 1, all_tiles, 0, SCALAR_GROUPS)
        deal(nc.vector.tensor_copy, w1_grouped, w1_raw[1], 1, all_tiles, SCALAR_GROUPS, P // 2)
        w1_codes = sb.tile([P, H], U32, name="w1_codes", align_bytes=MX_ALIGN)
        w1_scales = sb.tile([P, H], U8, name="w1_scales", align_bytes=MX_ALIGN)
        for t0, t1 in ((0, 1), (1, 2), (2, 4)):
            quantize(w1_codes[:, t0 * P : t1 * P], w1_scales[:, t0 * P : t1 * P], w1_grouped[:, t0:t1, :, :].rearrange("p t m j -> p (t m j)"))

        w2_raw = [load_half(w2, h) for h in range(2)]

        split = [ps.tile([P, S], F32, name=f"split{h}") for h in range(2)]
        y_banks = [[split[h][:, half(0)] for h in range(2)]] + [[ps.tile([P, S], F32, name=f"y_bank{t}")[:]] for t in (1, 2, 3)]
        h_banks = {t: [ps.tile([P, S], F32, name=f"h_bank{t}")[:]] for t in (3, 0, 1)}
        h_banks[2] = [split[h][:, half(1)] for h in range(2)]

        ds = [sb.tile([P, S], F32, name=f"ds{t}") for t in range(PACK)]
        y_tile = [sb.tile([P, 2 * S], F32, name=f"y_tile{t}") for t in range(PACK)]
        y = [tile[:, WHOLE] for tile in y_tile]
        for h in range(2):
            product(y_banks[0][h], w1_codes, w1_scales, 0, x_codes[:, half(h)], x_bytes[:, half(h)])
            nc.scalar.copy(ds[0][:, half(h)], y_banks[0][h])
        for t in (1, 2, 3):
            product(y_banks[t][0], w1_codes, w1_scales, t, x_codes[:], x_bytes[:])

        pa = [tile[:, S : S + W] for tile in y_tile[:3]] + [sb.tile([P, W], F32, name="pa3", align_bytes=MX_ALIGN)[:]]
        gate = [tile[:, S + W : 2 * S] for tile in y_tile[:3]] + [sb.tile([P, W], F32, name="gate3", align_bytes=MX_ALIGN)[:]]
        z_flat = sb.tile([P, PACK * S], BF16, name="z_flat")
        z_pairs = z_flat[:].rearrange("p (h u j e) -> p h u j e", h=2, u=2, e=2)

        def fetch(t):
            if t > 0:
                empty(ds[t], y_banks[t], 1.0)
            if t >= 2:
                nc.sync.dma_start(y[t], ds[t][:])
            nc.vector.tensor_copy(pa[t], ds[t][:].indirect(n1_t[:]))

        def make_gate(t):
            nc.scalar.activation(gate[t], ds[t][:].indirect(n2_t[:]), SIGMOID)

        def put(t):
            nc.vector.tensor_tensor(ds[t][:].indirect(n2_t[:]), pa[t], gate[t], MULT)

        def cast(t, halves):
            nc.scalar.activation(z_pairs[:, halves, t // 2, :, t % 2], ds[t][:].rearrange("p (h j) -> p h j", h=2)[:, halves, :], COPY, scale=gain[:, t : t + 1])

        def deal_w2(tiles, tag):
            grouped = sb.tile([P, 2, P, PACK], BF16, name="grouped", tag=tag, align_bytes=MX_ALIGN)
            for h in range(2):
                deal(nc.scalar.copy, grouped, w2_raw[h], h, tiles, 0, P // 2)
            return grouped

        def quantize_w2(grouped, tag):
            codes = sb.tile([P, 2 * P], U32, name="codes", tag=tag, align_bytes=MX_ALIGN)
            scales = sb.tile([P, 2 * P], U8, name="scales", tag=tag + "_scales", align_bytes=MX_ALIGN)
            quantize(codes[:], scales[:], grouped[:].rearrange("p t m j -> p (t m j)"))
            return codes, scales

        both = slice(0, 2)
        fetch(0)
        make_gate(0)
        put(0)
        fetch(1)
        fetch(2)
        make_gate(1)
        put(1)
        fetch(3)
        make_gate(2)
        cast(0, both)
        make_gate(3)
        cast(1, both)
        w2_early = deal_w2(slice(2, 4), "w2_early")
        put(2)
        cast(2, both)
        put(3)
        early_codes, early_scales = quantize_w2(w2_early, "pa3")
        for h in range(2):
            cast(3, slice(h, h + 1))
        w2_late = deal_w2(slice(0, 2), "gate3")

        h_tile = [sb.tile([P, S if t == 1 else 2 * S], F32, name=f"h_tile{t}", align_bytes=MX_ALIGN) for t in range(PACK)]
        hs = [tile[:, WHOLE] for tile in h_tile]
        z_words = [h_tile[2][:, SPARE].bitcast(I32), sb.tile([P, S], I32, name="z_words1", align_bytes=MX_ALIGN)[:]]
        z_codes = sb.tile([P, S], U32, name="z_codes", align_bytes=MX_ALIGN)
        z_scales = sb.tile([P, S], U8, name="z_scales", align_bytes=MX_ALIGN)
        for h in range(2):
            pairs = z_flat[:, h * 2 * S : (h + 1) * 2 * S].bitcast(I32)
            nc.vector.tensor_copy(z_words[h].rearrange("p (j u) -> p j u", u=2), pairs.rearrange("p (u j) -> p j u", u=2))
        for h in range(2):
            quantize(z_codes[:, half(h)], z_scales[:, half(h)], z_words[h].bitcast(BF16))
            product(h_banks[2][h], early_codes, early_scales, 0, z_codes[:, half(h)], z_scales[:, half(h)])
            nc.scalar.activation(hs[2][:, half(h)], h_banks[2][h], COPY, scale=OUT_SCALE)
        y2_picked = h_tile[2][:, SPARE]
        nc.vector.tensor_copy(y2_picked, y_tile[2][:].indirect(n4_t[:]))
        product(h_banks[3][0], early_codes, early_scales, 1, z_codes[:], z_scales[:])
        late_codes, late_scales = quantize_w2(w2_late, "late_codes")
        for t in (0, 1):
            product(h_banks[t][0], late_codes, late_scales, t, z_codes[:], z_scales[:])

        left = {t: sb.tile([P, S], F32, name=f"left{t}")[:] for t in (0, 1)}
        left[2], left[3] = y_tile[3][:, SPARE], h_tile[0][:, SPARE]
        right = {t: sb.tile([P, S], F32, name=f"right{t}")[:] for t in (3, 0, 1)}
        right[2] = h_tile[3][:, SPARE]
        neg_y = {t: sb.tile([P, S], F32, name=f"neg_y{t}")[:] for t in (2, 3)}
        turned = {t: sb.tile([P, S], F32, name=f"turned{t}") for t in (2, 3)}
        res = [sb.tile([P, S], F32, name=f"res{t}") for t in range(PACK)]
        out_rows = out.rearrange("(p t) j -> p t j", t=PACK)

        def make_left(t):
            nc.vector.tensor_tensor(left[t], y_tile[t][:].indirect(n4_t[:]), hs[t], MULT)

        def make_right(t, c, factor):
            nc.vector.tensor_tensor(right[t][:, c], h_tile[t][:].indirect(entries(n3_t, c)), factor[:, c], MULT)

        def subtract(t, c):
            nc.vector.tensor_tensor(res[t][:, c], left[t][:, c], right[t][:, c], SUB)
            nc.sync.dma_start(out_rows[:, t, c], res[t][:, c])

        def add_turned(t, h):
            acc = ps.tile([P, HALF], F32, name="acc", tag=("y_bank2", "y_bank3")[h])
            for b in range(0, HALF, P):
                block = slice(h * HALF + b, h * HALF + b + P)
                nc.tensor.matmul(acc[:, b : b + P], left[t][:, block], ident[:], start=True, stop=False, is_transpose=True)
                nc.tensor.matmul(acc[:, b : b + P], right[t][:, block], ident[:], start=False, stop=True, is_transpose=True)
            nc.scalar.copy(turned[t][:, half(h)], acc[:])

        def turn_back(t, h):
            back = ps.tile([P, HALF], F32, name="back", tag=("h_bank3", "split0")[h])
            for b in range(0, HALF, P):
                nc.tensor.transpose(back[:, b : b + P], turned[t][:, h * HALF + b : h * HALF + b + P], ident[:])
            nc.scalar.copy(res[t][:, half(h)], back[:])
            nc.scalar.dma_start(out_rows[:, t, half(h)], res[t][:, half(h)])

        def add_up(t):
            for h in range(2):
                add_turned(t, h)
            for h in range(2):
                turn_back(t, h)

        empty(neg_y[2], y_banks[2], -1.0)
        nc.vector.tensor_tensor(left[2], y2_picked, hs[2], MULT)
        make_right(2, WHOLE, neg_y[2])

        empty(hs[3], h_banks[3], OUT_SCALE)
        empty(neg_y[3], y_banks[3], -1.0)
        make_left(3)
        make_right(3, WHOLE, neg_y[3])

        empty(y[0], y_banks[0], 1.0)
        empty(hs[0], h_banks[0], OUT_SCALE)
        empty(y[1], y_banks[1], 1.0)
        empty(hs[1], h_banks[1], OUT_SCALE)
        add_up(2)
        make_left(0)
        make_right(0, WHOLE, y[0])
        add_up(3)

        wide, narrow = slice(0, S - P), slice(S - P, S)
        make_left(1)
        subtract(0, WHOLE)
        make_right(1, wide, y[1])
        make_right(1, narrow, y[1])
        subtract(1, wide)
        subtract(1, narrow)
